import numpy as np
import ml_dtypes


def mxq(x, axis, fmt="e4m3"):
    dtype, down = {"e4m3": (ml_dtypes.float8_e4m3fn, 7), "e5m2": (ml_dtypes.float8_e5m2, 14)}[fmt]
    v = np.moveaxis(np.asarray(x, np.float32).astype(ml_dtypes.bfloat16).astype(np.float64), axis, -1)
    blocks = v.reshape(v.shape[:-1] + (-1, 32))
    amax = np.abs(blocks).max(-1, keepdims=True)
    byte = np.maximum(np.where(amax > 0, np.frexp(amax)[1] - 1 + 127, 0) - down, 1)
    scale = np.exp2(byte - 127.0)
    codes = (blocks / scale).astype(np.float32).astype(dtype).astype(np.float64)
    return np.moveaxis((codes * scale).reshape(v.shape), -1, axis)


WIDE = False


def mx_kscale(k):
    if not WIDE:
        return np.ones(k)
    levels = np.array([10, -10, 5, -5, 0])
    if k % 512:
        return np.exp2(np.random.permutation(np.resize(levels, k // 32))).repeat(32)
    a = np.empty((k // 512, 16))
    for p in range(k // 512):
        a[p, :8] = np.random.permutation(np.resize(levels, 8))
        for g in range(8):
            far = levels[np.abs(levels - a[p, g]) >= 10]
            a[p, g + 8] = far[np.random.randint(len(far))]
    return np.exp2(a.ravel()).repeat(32)


def f64(x):
    return np.asarray(x).astype(np.float64)


def striped(idx):
    return np.tile(np.asarray(idx).reshape(-1, 16).T, (8, 1)).astype(np.uint16)


def unstriped(offs):
    return offs[:16].T.reshape(-1).astype(np.int64)


E2M1 = np.array([0.0, 0.5, 1.0, 1.5, 2.0, 3.0, 4.0, 6.0, -0.0, -0.5, -1.0, -1.5, -2.0, -3.0, -4.0, -6.0])


def pack_weight(w, fmt):
    k, n = w.shape
    w = f64(np.asarray(w, np.float32).astype(ml_dtypes.bfloat16)).reshape(k // 32, 32, n)
    amax = np.abs(w).max(1)
    if fmt == "e4m3":
        byte = np.frexp(amax)[1] - 1 + 127 - 7
    else:
        mant, ex = np.frexp(amax / 6.0)
        byte = np.where(mant > 0.5, ex, ex - 1) + 127
    byte = np.clip(np.where(amax > 0, byte, 1), 1, 254)
    scaled = (w * np.exp2(127.0 - byte)[:, None, :]).reshape(k, n).astype(np.float32)
    by_word = np.ascontiguousarray(scaled.reshape(k // 512, 128, 4, n).transpose(0, 1, 3, 2))
    if fmt == "e4m3":
        words = by_word.astype(ml_dtypes.float8_e4m3fn).view(np.uint8)
    else:
        c = by_word.astype(ml_dtypes.float4_e2m1fn).view(np.uint8) & 0xF
        words = (c[..., 0::2] | (c[..., 1::2] << 4)).reshape(k // 512, 128, 2 * n)
    return np.ascontiguousarray(words), np.ascontiguousarray(byte.astype(np.uint8).reshape(k // 512, 16, n))


def unpack_weight(words, scales, fmt):
    g, _, n = scales.shape
    words = np.ascontiguousarray(words).reshape(g, 128, n, -1)
    if fmt == "e4m3":
        vals = words.view(ml_dtypes.float8_e4m3fn).astype(np.float64)
    else:
        nib = np.empty((g, 128, n, 4), np.uint8)
        nib[..., 0::2] = words & 0xF
        nib[..., 1::2] = words >> 4
        vals = E2M1[nib]
    vals = vals * np.repeat(np.exp2(scales.astype(np.float64) - 127.0), 8, axis=1)[..., None]
    return vals.transpose(0, 1, 3, 2).reshape(g * 512, n)


def rot(x):
    y = x.reshape(-1, 2, x.shape[1])
    return np.stack([-y[:, 1], y[:, 0]], axis=1).reshape(x.shape)


D, E, T, I, U, V, Q = 512, 512, 2048, 256, 1024, 512, 512


def setup_inputs():
    n = np.random.standard_normal
    idx = np.random.permutation(T)[:I]
    idx2 = np.random.randint(0, V, I)
    idx3 = np.random.permutation(U)[:I]
    fd = mx_kscale(D)
    fq = mx_kscale(Q)
    keysp = pack_weight(n((D, T)) / fd[:, None], "e4m3")
    return {
        "query": (n((D, Q)) * 0.5 / np.sqrt(D) * fd[:, None]).astype(np.float32),
        "keys_words": keysp[0],
        "keys_scales": keysp[1],
        "qs": (np.random.uniform(8.0, 32.0, (Q, 1)) * fq[:, None]).astype(np.float32),
        "grows": (n((Q, E)) / fq[:, None]).astype(np.float32),
        "cosn": (np.repeat(np.round(np.cos(np.arange(E // 2)[:, None] * 0.11 + np.arange(V)[None] * 0.37) * 64) / 64, 2, axis=0)).astype(np.float32),
        "sinn": (np.repeat(np.round(np.sin(np.arange(E // 2)[:, None] * 0.11 + np.arange(V)[None] * 0.37) * 64) / 64, 2, axis=0)).astype(np.float32),
        "old": (n((E, U)) * 2.0).astype(np.float32),
        "offs": striped(idx),
        "offs2": striped(idx2),
        "offs3": striped(idx3),
    }


def reference(query, keys_words, keys_scales, qs, grows, cosn, sinn, old, offs, offs2, offs3):
    idx = unstriped(offs)
    idx2 = unstriped(offs2)
    idx3 = unstriped(offs3)
    keysu = unpack_weight(keys_words, keys_scales, "e4m3")
    queryq = mxq(f64(query), 0, "e4m3")
    keysidxg = keysu[:, idx]
    a = queryq.T @ keysidxg
    p = np.exp(a - np.max(a, axis=1, keepdims=True))
    w = p * f64(qs) / np.sum(p, axis=1, keepdims=True)
    growsq = mxq(f64(grows), 0, "e4m3")
    wq = mxq(w, 0, "e4m3")
    dv = growsq.T @ wq
    dr = rot(dv)
    db = dv * f64(cosn)[:, idx2] - dr * f64(sinn)[:, idx2]
    vf = np.zeros((E, U))
    vf[:, idx3] = db
    y = f64(old) + vf
    return y

@@ -1,0 +1,161 @@
+from contextlib import ExitStack
+
+import concourse.mybir as mybir
+
+D, E, T, I, U, V, Q = 512, 512, 2048, 256, 1024, 512, 512
+FLOPS = 2 * D * Q * I + 2 * Q * E * I
+
+F32 = mybir.dt.float32
+BF16 = mybir.dt.bfloat16
+I32 = mybir.dt.int32
+U32 = mybir.dt.uint32
+U16 = mybir.dt.uint16
+U8 = mybir.dt.uint8
+FP8X4 = mybir.dt.float8_e4m3fn_x4
+ALU = mybir.AluOpType
+ACT = mybir.ActivationFunctionType
+AX = mybir.AxisListType
+
+P = 128
+PACK = 4
+HALVES = 2
+EH = E // HALVES
+
+
+def tile_attend_gturnedvalues_kernel(tc, query, keys_words, keys_scales, qs, grows, cosn, sinn, old,
+                                      offs, offs2, offs3, out):
+    nc = tc.nc
+    with ExitStack() as ctx:
+        sb = ctx.enter_context(tc.tile_pool(name="sb", bufs=1))
+        ps = ctx.enter_context(tc.psum_pool(name="ps", bufs=1))
+
+        key_list = sb.tile([P, I // 16], U16, name="key_list")
+        dist_list = sb.tile([P, I // 16], U16, name="dist_list")
+        place_list = sb.tile([P, I // 16], U16, name="place_list")
+        pool_scales = sb.tile([P, T], U8, name="pool_scales", align_bytes=64)
+        pool_words = sb.tile([P, T], U32, name="pool_words", align_bytes=64)
+        q_raw = sb.tile([P, PACK, Q], F32, name="q_raw", align_bytes=64)
+        row_scale = sb.tile([P, PACK], F32, name="row_scale")
+        g_raw = [sb.tile([P, PACK, EH], F32, name="g_raw%d" % h, align_bytes=64) for h in range(HALVES)]
+        cos_tab = [sb.tile([P, V], F32, name="cos_tab%d" % h, align_bytes=64) for h in range(HALVES)]
+        sin_tab = [sb.tile([P, V], F32, name="sin_tab%d" % h, align_bytes=64) for h in range(HALVES)]
+        old_sb = [[sb.tile([P, U], F32, name="old%d%d" % (h, j), align_bytes=64) for j in range(2)] for h in range(HALVES)]
+        placed = [[sb.tile([P, U], F32, name="placed%d%d" % (h, j), align_bytes=64) for j in range(2)] for h in range(HALVES)]
+
+        warm_in = sb.tile([P, 1], F32, name="warm_in")
+        warm_out = sb.tile([P, 1], F32, name="warm_out")
+
+        nc.vector.memset(pool_scales[:].bitcast(I32), 0)
+        nc.gpsimd.memset(warm_in[:], 0.0)
+        for quad in range(4):
+            nc.scalar.dma_start(out=pool_scales[32 * quad:32 * quad + 4, :].bitcast(I32),
+                                in_=keys_scales[0, 4 * quad:4 * quad + 4, :].bitcast(I32))
+        nc.scalar.activation(out=warm_out[:], in_=warm_in[:], func=ACT.Exp)
+
+        nc.sync.dma_start(out=q_raw[:], in_=query.rearrange("(p j) q -> p j q", j=PACK))
+        nc.sync.dma_start(key_list[:], offs)
+        nc.sync.dma_start(out=pool_words[:].bitcast(I32),
+                          in_=keys_words[0].rearrange("p t r -> p (t r)").bitcast(I32))
+        g_rows = grows.rearrange("(p r) e -> p r e", r=PACK)
+        cos_rows = cosn.rearrange("(h p j) v -> h j p v", h=HALVES, j=2)
+        sin_rows = sinn.rearrange("(h p j) v -> h j p v", h=HALVES, j=2)
+        old_rows = old.rearrange("(h p j) u -> h j p u", h=HALVES, j=2)
+        out_rows = out.rearrange("(h p j) u -> h j p u", h=HALVES, j=2)
+        nc.sync.dma_start(out=g_raw[0][:], in_=g_rows[:, :, 0:EH])
+        nc.sync.dma_start(out=row_scale[:], in_=qs.rearrange("(p r) o -> p (r o)", r=PACK))
+        nc.sync.dma_start(dist_list[:], offs2)
+        nc.sync.dma_start(out=cos_tab[0][:], in_=cos_rows[0, 0])
+        nc.sync.dma_start(out=sin_tab[0][:], in_=sin_rows[0, 0])
+        nc.sync.dma_start(place_list[:], offs3)
+        nc.sync.dma_start(out=g_raw[1][:], in_=g_rows[:, :, EH:E])
+        nc.sync.dma_start(out=cos_tab[1][:], in_=cos_rows[1, 0])
+        nc.sync.dma_start(out=sin_tab[1][:], in_=sin_rows[1, 0])
+        for h in range(HALVES):
+            for j in range(2):
+                nc.sync.dma_start(out=old_sb[h][j][:], in_=old_rows[h, j])
+
+        for h in range(HALVES):
+            for j in range(2):
+                nc.vector.memset(placed[h][j][:], 0.0)
+
+        key_scales = sb.tile([P, I], U8, name="key_scales", align_bytes=64)
+        nc.vector.tensor_copy(key_scales[:], pool_scales[:].indirect(key_list[:]))
+
+        q_bf = sb.tile([P, PACK, P, PACK], BF16, name="q_bf", align_bytes=64)
+        nc.vector.tensor_copy(out=q_bf[:].rearrange("p r s j -> p s j r"),
+                              in_=q_raw[:].rearrange("p j (s r) -> p s j r", r=PACK))
+        q_codes = sb.tile([P, Q], U32, name="q_codes", align_bytes=64)
+        q_scales = sb.tile([P, Q], U8, name="q_scales", align_bytes=64)
+        nc.vector.quantize_mx(out=q_codes[:].bitcast(FP8X4), scales=q_scales[:],
+                              in_=q_bf[:].rearrange("p r s j -> p (r s j)"))
+
+        key_words = sb.tile([P, I], U32, name="key_words", align_bytes=64)
+        nc.vector.tensor_copy(key_words[:], pool_words[:].indirect(key_list[:]))
+
+        neg_max = sb.tile([P, PACK], F32, name="neg_max")
+        row_sum = sb.tile([P, PACK], F32, name="row_sum")
+        probs = sb.tile([P, PACK, I], F32, name="probs", align_bytes=64)
+        for r in range(PACK):
+            cols = slice(r * P, (r + 1) * P)
+            scores = ps.tile([P, I], F32, name="scores%d" % r)
+            nc.tensor.matmul_mx(out=scores[:], lhsT=q_codes[:, cols].bitcast(FP8X4), lhsT_scale=q_scales[:, cols],
+                                rhs=key_words[:].bitcast(FP8X4), rhs_scale=key_scales[:], start=True, stop=True)
+            nc.vector.tensor_reduce(out=neg_max[:, r:r + 1], in_=scores[:], axis=AX.X, op=ALU.max, negate=True)
+            nc.scalar.activation(out=probs[:, r, :], in_=scores[:], func=ACT.Exp, bias=neg_max[:, r:r + 1],
+                                 accum_out=row_sum[:, r:r + 1])
+
+        g_bf, g_codes, g_scales = [], [], []
+        for h in range(HALVES):
+            g_bf.append(sb.tile([P, 2, P, PACK], BF16, name="g_bf%d" % h, align_bytes=64))
+            g_codes.append(sb.tile([P, EH], U32, name="g_codes%d" % h, align_bytes=64))
+            g_scales.append(sb.tile([P, EH], U8, name="g_scales%d" % h, align_bytes=64))
+            nc.scalar.copy(out=g_bf[h][:].rearrange("p j (c m) r -> p c r m j", m=2),
+                           in_=g_raw[h][:].rearrange("p r (c m j) -> p c r m j", m=2, j=2))
+
+        inv_sum = sb.tile([P, PACK], F32, name="inv_sum")
+        factor = sb.tile([P, PACK], F32, name="factor")
+        nc.vector.reciprocal(out=inv_sum[:], in_=row_sum[:])
+        nc.vector.tensor_tensor(out=factor[:], in0=inv_sum[:], in1=row_scale[:], op=ALU.mult)
+        w_bf = sb.tile([P, I, PACK], BF16, name="w_bf", align_bytes=64)
+        nc.vector.tensor_tensor(out=w_bf[:].rearrange("p (c m) r -> p c r m", m=4),
+                                in0=probs[:].rearrange("p r (c m) -> p c r m", m=4),
+                                in1=factor[:].unsqueeze(1).unsqueeze(3).to_broadcast([P, I // 4, PACK, 4]),
+                                op=ALU.mult)
+        w_codes = sb.tile([P, I], U32, name="w_codes", align_bytes=64)
+        w_scales = sb.tile([P, I], U8, name="w_scales", align_bytes=64)
+
+        def quantise_grows(h):
+            nc.vector.quantize_mx(out=g_codes[h][:].bitcast(FP8X4), scales=g_scales[h][:],
+                                  in_=g_bf[h][:].rearrange("p j s r -> p (j s r)"))
+
+        quantise_grows(0)
+        nc.vector.quantize_mx(out=w_codes[:].bitcast(FP8X4), scales=w_scales[:],
+                              in_=w_bf[:].rearrange("p i r -> p (i r)"))
+
+        for h in range(HALVES):
+            if h > 0:
+                quantise_grows(h)
+            dv = ps.tile([P, 2, I], F32, name="dv%d" % h)
+            for j in range(2):
+                cols = slice(j * P, (j + 1) * P)
+                nc.tensor.matmul_mx(out=dv[:, j, :], lhsT=g_codes[h][:, cols].bitcast(FP8X4),
+                                    lhsT_scale=g_scales[h][:, cols], rhs=w_codes[:].bitcast(FP8X4),
+                                    rhs_scale=w_scales[:], start=True, stop=True)
+            cos_g = sb.tile([P, I], F32, name="cos_g%d" % h, align_bytes=64)
+            sin_g = sb.tile([P, I], F32, name="sin_g%d" % h, align_bytes=64)
+            nc.vector.tensor_copy(cos_g[:], cos_tab[h][:].indirect(dist_list[:]))
+            nc.vector.tensor_copy(sin_g[:], sin_tab[h][:].indirect(dist_list[:]))
+            by_cos = sb.tile([P, 2, I], F32, name="by_cos%d" % h, align_bytes=64)
+            by_sin = sb.tile([P, 2, I], F32, name="by_sin%d" % h, align_bytes=64)
+            nc.vector.tensor_tensor(out=by_cos[:], in0=dv[:], in1=cos_g[:].unsqueeze(1).to_broadcast([P, 2, I]),
+                                    op=ALU.mult)
+            nc.vector.tensor_tensor(out=by_sin[:, 0, :], in0=dv[:, 1, :], in1=sin_g[:], op=ALU.mult)
+            nc.vector.scalar_tensor_tensor(out=by_sin[:, 1, :], in0=dv[:, 0, :], scalar=-1.0, in1=sin_g[:],
+                                           op0=ALU.mult, op1=ALU.mult)
+            for j in range(2):
+                nc.vector.tensor_tensor(placed[h][j][:].indirect(place_list[:]), by_cos[:, j, :], by_sin[:, j, :],
+                                        ALU.add)
+            for j in range(2):
+                total = sb.tile([P, U], F32, name="total%d%d" % (h, j), align_bytes=64)
+                nc.vector.tensor_tensor(out=total[:], in0=placed[h][j][:], in1=old_sb[h][j][:], op=ALU.add)
+                nc.sync.dma_start(out=out_rows[h, j], in_=total[:])

@@ -1,6 +1,7 @@
 from contextlib import ExitStack
 
 import concourse.mybir as mybir
+from concourse.masks import make_identity
 
 D, E, T, I, U, V, Q = 512, 512, 2048, 256, 1024, 512, 512
 FLOPS = 2 * D * Q * I + 2 * Q * E * I
@@ -45,14 +46,13 @@ def tile_attend_gturnedvalues_kernel(tc, query, keys_words, keys_scales, qs, gro
         warm_in = sb.tile([P, 1], F32, name="warm_in")
         warm_out = sb.tile([P, 1], F32, name="warm_out")
 
-        nc.vector.memset(pool_scales[:].bitcast(I32), 0)
+        nc.gpsimd.memset(pool_scales[:].bitcast(I32), 0)
         nc.gpsimd.memset(warm_in[:], 0.0)
-        for quad in range(4):
-            nc.scalar.dma_start(out=pool_scales[32 * quad:32 * quad + 4, :].bitcast(I32),
-                                in_=keys_scales[0, 4 * quad:4 * quad + 4, :].bitcast(I32))
         nc.scalar.activation(out=warm_out[:], in_=warm_in[:], func=ACT.Exp)
 
         nc.sync.dma_start(out=q_raw[:], in_=query.rearrange("(p j) q -> p j q", j=PACK))
+        for r in range(4):
+            nc.sync.dma_start(out=pool_scales[r:P:32, :].bitcast(I32), in_=keys_scales[0, r:16:4, :].bitcast(I32))
         nc.sync.dma_start(key_list[:], offs)
         nc.sync.dma_start(out=pool_words[:].bitcast(I32),
                           in_=keys_words[0].rearrange("p t r -> p (t r)").bitcast(I32))
@@ -61,33 +61,37 @@ def tile_attend_gturnedvalues_kernel(tc, query, keys_words, keys_scales, qs, gro
         sin_rows = sinn.rearrange("(h p j) v -> h j p v", h=HALVES, j=2)
         old_rows = old.rearrange("(h p j) u -> h j p u", h=HALVES, j=2)
         out_rows = out.rearrange("(h p j) u -> h j p u", h=HALVES, j=2)
-        nc.sync.dma_start(out=g_raw[0][:], in_=g_rows[:, :, 0:EH])
-        nc.sync.dma_start(out=row_scale[:], in_=qs.rearrange("(p r) o -> p (r o)", r=PACK))
-        nc.sync.dma_start(dist_list[:], offs2)
         nc.sync.dma_start(out=cos_tab[0][:], in_=cos_rows[0, 0])
+        nc.sync.dma_start(dist_list[:], offs2)
         nc.sync.dma_start(out=sin_tab[0][:], in_=sin_rows[0, 0])
-        nc.sync.dma_start(place_list[:], offs3)
+        nc.sync.dma_start(out=row_scale[:], in_=qs.rearrange("(p r) o -> p (r o)", r=PACK))
+        nc.sync.dma_start(out=g_raw[0][:], in_=g_rows[:, :, 0:EH])
         nc.sync.dma_start(out=g_raw[1][:], in_=g_rows[:, :, EH:E])
+        nc.sync.dma_start(place_list[:], offs3)
         nc.sync.dma_start(out=cos_tab[1][:], in_=cos_rows[1, 0])
         nc.sync.dma_start(out=sin_tab[1][:], in_=sin_rows[1, 0])
         for h in range(HALVES):
             for j in range(2):
                 nc.sync.dma_start(out=old_sb[h][j][:], in_=old_rows[h, j])
 
+        ident = sb.tile([P, P], F32, name="ident", align_bytes=64)
+        make_identity(nc, ident[:])
         for h in range(HALVES):
             for j in range(2):
                 nc.vector.memset(placed[h][j][:], 0.0)
 
+        q_cols = q_raw[:].rearrange("p j (s r) -> p s j r", r=PACK)
+        q_codes, q_scales, q_bf = [], [], []
+        for a, copy in enumerate((nc.vector.tensor_copy, nc.scalar.copy)):
+            q_bf.append(sb.tile([P, 2, P, PACK], BF16, name="q_bf%d" % a, align_bytes=64))
+            copy(out=q_bf[a][:].rearrange("p r s j -> p s j r"), in_=q_cols[:, :, :, 2 * a:2 * a + 2])
         key_scales = sb.tile([P, I], U8, name="key_scales", align_bytes=64)
         nc.vector.tensor_copy(key_scales[:], pool_scales[:].indirect(key_list[:]))
-
-        q_bf = sb.tile([P, PACK, P, PACK], BF16, name="q_bf", align_bytes=64)
-        nc.vector.tensor_copy(out=q_bf[:].rearrange("p r s j -> p s j r"),
-                              in_=q_raw[:].rearrange("p j (s r) -> p s j r", r=PACK))
-        q_codes = sb.tile([P, Q], U32, name="q_codes", align_bytes=64)
-        q_scales = sb.tile([P, Q], U8, name="q_scales", align_bytes=64)
-        nc.vector.quantize_mx(out=q_codes[:].bitcast(FP8X4), scales=q_scales[:],
-                              in_=q_bf[:].rearrange("p r s j -> p (r s j)"))
+        for a in range(2):
+            q_codes.append(sb.tile([P, 2 * P], U32, name="q_codes%d" % a, align_bytes=64))
+            q_scales.append(sb.tile([P, 2 * P], U8, name="q_scales%d" % a, align_bytes=64))
+            nc.vector.quantize_mx(out=q_codes[a][:].bitcast(FP8X4), scales=q_scales[a][:],
+                                  in_=q_bf[a][:].rearrange("p r s j -> p (r s j)"))
 
         key_words = sb.tile([P, I], U32, name="key_words", align_bytes=64)
         nc.vector.tensor_copy(key_words[:], pool_words[:].indirect(key_list[:]))
@@ -96,9 +100,10 @@ def tile_attend_gturnedvalues_kernel(tc, query, keys_words, keys_scales, qs, gro
         row_sum = sb.tile([P, PACK], F32, name="row_sum")
         probs = sb.tile([P, PACK, I], F32, name="probs", align_bytes=64)
         for r in range(PACK):
-            cols = slice(r * P, (r + 1) * P)
-            scores = ps.tile([P, I], F32, name="scores%d" % r)
-            nc.tensor.matmul_mx(out=scores[:], lhsT=q_codes[:, cols].bitcast(FP8X4), lhsT_scale=q_scales[:, cols],
+            cols = slice(r % 2 * P, (r % 2 + 1) * P)
+            scores = ps.tile([P, I], F32, name="scores%d" % r, tag="bank%d" % r)
+            nc.tensor.matmul_mx(out=scores[:], lhsT=q_codes[r // 2][:, cols].bitcast(FP8X4),
+                                lhsT_scale=q_scales[r // 2][:, cols],
                                 rhs=key_words[:].bitcast(FP8X4), rhs_scale=key_scales[:], start=True, stop=True)
             nc.vector.tensor_reduce(out=neg_max[:, r:r + 1], in_=scores[:], axis=AX.X, op=ALU.max, negate=True)
             nc.scalar.activation(out=probs[:, r, :], in_=scores[:], func=ACT.Exp, bias=neg_max[:, r:r + 1],
@@ -112,6 +117,15 @@ def tile_attend_gturnedvalues_kernel(tc, query, keys_words, keys_scales, qs, gro
             nc.scalar.copy(out=g_bf[h][:].rearrange("p j (c m) r -> p c r m j", m=2),
                            in_=g_raw[h][:].rearrange("p r (c m j) -> p c r m j", m=2, j=2))
 
+        cos_g, sin_g = [], []
+
+        def gather_angles(h):
+            cos_g.append(sb.tile([P, I], F32, name="cos_g%d" % h, align_bytes=64))
+            sin_g.append(sb.tile([P, I], F32, name="sin_g%d" % h, align_bytes=64))
+            nc.vector.tensor_copy(cos_g[h][:], cos_tab[h][:].indirect(dist_list[:]))
+            nc.vector.tensor_copy(sin_g[h][:], sin_tab[h][:].indirect(dist_list[:]))
+
+        gather_angles(0)
         inv_sum = sb.tile([P, PACK], F32, name="inv_sum")
         factor = sb.tile([P, PACK], F32, name="factor")
         nc.vector.reciprocal(out=inv_sum[:], in_=row_sum[:])
@@ -132,30 +146,72 @@ def tile_attend_gturnedvalues_kernel(tc, query, keys_words, keys_scales, qs, gro
         nc.vector.quantize_mx(out=w_codes[:].bitcast(FP8X4), scales=w_scales[:],
                               in_=w_bf[:].rearrange("p i r -> p (i r)"))
 
-        for h in range(HALVES):
-            if h > 0:
-                quantise_grows(h)
-            dv = ps.tile([P, 2, I], F32, name="dv%d" % h)
+        dv = []
+
+        def second_product(h):
+            dv.append(ps.tile([P, 2, I], F32, name="dv%d" % h))
             for j in range(2):
                 cols = slice(j * P, (j + 1) * P)
-                nc.tensor.matmul_mx(out=dv[:, j, :], lhsT=g_codes[h][:, cols].bitcast(FP8X4),
+                nc.tensor.matmul_mx(out=dv[h][:, j, :], lhsT=g_codes[h][:, cols].bitcast(FP8X4),
                                     lhsT_scale=g_scales[h][:, cols], rhs=w_codes[:].bitcast(FP8X4),
                                     rhs_scale=w_scales[:], start=True, stop=True)
-            cos_g = sb.tile([P, I], F32, name="cos_g%d" % h, align_bytes=64)
-            sin_g = sb.tile([P, I], F32, name="sin_g%d" % h, align_bytes=64)
-            nc.vector.tensor_copy(cos_g[:], cos_tab[h][:].indirect(dist_list[:]))
-            nc.vector.tensor_copy(sin_g[:], sin_tab[h][:].indirect(dist_list[:]))
+
+        def turn_and_place(h):
             by_cos = sb.tile([P, 2, I], F32, name="by_cos%d" % h, align_bytes=64)
             by_sin = sb.tile([P, 2, I], F32, name="by_sin%d" % h, align_bytes=64)
-            nc.vector.tensor_tensor(out=by_cos[:], in0=dv[:], in1=cos_g[:].unsqueeze(1).to_broadcast([P, 2, I]),
-                                    op=ALU.mult)
-            nc.vector.tensor_tensor(out=by_sin[:, 0, :], in0=dv[:, 1, :], in1=sin_g[:], op=ALU.mult)
-            nc.vector.scalar_tensor_tensor(out=by_sin[:, 1, :], in0=dv[:, 0, :], scalar=-1.0, in1=sin_g[:],
+            nc.vector.tensor_tensor(out=by_cos[:], in0=dv[h][:],
+                                    in1=cos_g[h][:].unsqueeze(1).to_broadcast([P, 2, I]), op=ALU.mult)
+            nc.vector.tensor_tensor(out=by_sin[:, 0, :], in0=dv[h][:, 1, :], in1=sin_g[h][:], op=ALU.mult)
+            nc.vector.scalar_tensor_tensor(out=by_sin[:, 1, :], in0=dv[h][:, 0, :], scalar=-1.0, in1=sin_g[h][:],
                                            op0=ALU.mult, op1=ALU.mult)
             for j in range(2):
                 nc.vector.tensor_tensor(placed[h][j][:].indirect(place_list[:]), by_cos[:, j, :], by_sin[:, j, :],
                                         ALU.add)
-            for j in range(2):
-                total = sb.tile([P, U], F32, name="total%d%d" % (h, j), align_bytes=64)
-                nc.vector.tensor_tensor(out=total[:], in0=placed[h][j][:], in1=old_sb[h][j][:], op=ALU.add)
-                nc.sync.dma_start(out=out_rows[h, j], in_=total[:])
+
+        turned_ps = {}
+
+        def turn_blocks(h, j, b, source, opens):
+            for k in range(4):
+                c0 = (4 * b + k) * P
+                nc.tensor.matmul(turned_ps[h, j, b][:, k, :], lhsT=source[:, c0:c0 + P], rhs=ident[:], is_transpose=True,
+                                 start=(opens and k == 0), stop=(not opens and k == 3))
+
+        def turn_old(h, j, b):
+            turned_ps[h, j, b] = ps.tile([P, 4, P], F32, name="turned_ps", tag="bank%d" % (2 * j + b))
+            turn_blocks(h, j, b, old_sb[h][j], True)
+
+        def add_on_tensor(h, j, halves):
+            turned = {}
+            for b in halves:
+                turn_blocks(h, j, b, placed[h][j], False)
+                turned[b] = sb.tile([P, 4, P], F32, name="turned", tag="turned", bufs=2, align_bytes=64)
+                nc.scalar.copy(out=turned[b][:], in_=turned_ps[h, j, b][:])
+            for b in halves:
+                back_ps = ps.tile([P, 4, P], F32, name="back_ps", tag="back", bufs=2)
+                for k in range(4):
+                    nc.tensor.transpose(back_ps[:, k, :], turned[b][:, k, :], ident[:])
+                total = sb.tile([P, 4 * P], F32, name="total_t%d%d%d" % (h, j, b), align_bytes=64)
+                nc.scalar.copy(out=total[:], in_=back_ps[:].rearrange("p k c -> p (k c)"))
+                nc.scalar.dma_start(out=out_rows[h, j][:, b * 512:(b + 1) * 512], in_=total[:])
+
+        def add_on_vector(h, j, bounds):
+            for lo, hi in zip(bounds, bounds[1:]):
+                total = sb.tile([P, hi - lo], F32, name="total_v%d%d_%d" % (h, j, lo), align_bytes=64)
+                nc.vector.tensor_tensor(out=total[:], in0=placed[h][j][:, lo:hi], in1=old_sb[h][j][:, lo:hi], op=ALU.add)
+                nc.sync.dma_start(out=out_rows[h, j][:, lo:hi], in_=total[:])
+
+        second_product(0)
+        gather_angles(1)
+        quantise_grows(1)
+        second_product(1)
+        turn_and_place(0)
+        for j in range(2):
+            for b in range(2):
+                turn_old(0, j, b)
+        add_on_tensor(0, 0, (0, 1))
+        turn_old(1, 0, 0)
+        add_on_tensor(0, 1, (0, 1))
+        turn_and_place(1)
+        add_on_tensor(1, 0, (0,))
+        add_on_vector(1, 0, (512, 1024))
+        add_on_vector(1, 1, (0, 512, 768, 1024))

@@ -38,9 +38,11 @@ def tile_attend_gturnedvalues_kernel(tc, query, keys_words, keys_scales, qs, gro
         q_raw = sb.tile([P, PACK, Q], F32, name="q_raw", align_bytes=64)
         row_scale = sb.tile([P, PACK], F32, name="row_scale")
         g_raw = [sb.tile([P, PACK, EH], F32, name="g_raw%d" % h, align_bytes=64) for h in range(HALVES)]
-        cos_tab = [sb.tile([P, V], F32, name="cos_tab%d" % h, align_bytes=64) for h in range(HALVES)]
+        cos_tab = [sb.tile([P, V], F32, name="cos_tab%d" % h, tag=("cos0_then_max", "cos1")[h], align_bytes=64)
+                   for h in range(HALVES)]
         sin_tab = [sb.tile([P, V], F32, name="sin_tab%d" % h, align_bytes=64) for h in range(HALVES)]
-        old_sb = [[sb.tile([P, U], F32, name="old%d%d" % (h, j), align_bytes=64) for j in range(2)] for h in range(HALVES)]
+        old_half = [[sb.tile([P, U // 2], F32, name="old0%d%d" % (j, b), tag="old0%d%d" % (j, b), align_bytes=64) for b in range(2)] for j in range(2)]
+        old_sb = [sb.tile([P, U], F32, name="old1%d" % j, align_bytes=64) for j in range(2)]
         placed = [[sb.tile([P, U], F32, name="placed%d%d" % (h, j), align_bytes=64) for j in range(2)] for h in range(HALVES)]
 
         warm_in = sb.tile([P, 1], F32, name="warm_in")
@@ -54,6 +56,7 @@ def tile_attend_gturnedvalues_kernel(tc, query, keys_words, keys_scales, qs, gro
         for r in range(4):
             nc.sync.dma_start(out=pool_scales[r:P:32, :].bitcast(I32), in_=keys_scales[0, r:16:4, :].bitcast(I32))
         nc.sync.dma_start(key_list[:], offs)
+        nc.sync.dma_start(dist_list[:], offs2)
         nc.sync.dma_start(out=pool_words[:].bitcast(I32),
                           in_=keys_words[0].rearrange("p t r -> p (t r)").bitcast(I32))
         g_rows = grows.rearrange("(p r) e -> p r e", r=PACK)
@@ -62,17 +65,19 @@ def tile_attend_gturnedvalues_kernel(tc, query, keys_words, keys_scales, qs, gro
         old_rows = old.rearrange("(h p j) u -> h j p u", h=HALVES, j=2)
         out_rows = out.rearrange("(h p j) u -> h j p u", h=HALVES, j=2)
         nc.sync.dma_start(out=cos_tab[0][:], in_=cos_rows[0, 0])
-        nc.sync.dma_start(dist_list[:], offs2)
         nc.sync.dma_start(out=sin_tab[0][:], in_=sin_rows[0, 0])
         nc.sync.dma_start(out=row_scale[:], in_=qs.rearrange("(p r) o -> p (r o)", r=PACK))
-        nc.sync.dma_start(out=g_raw[0][:], in_=g_rows[:, :, 0:EH])
-        nc.sync.dma_start(out=g_raw[1][:], in_=g_rows[:, :, EH:E])
         nc.sync.dma_start(place_list[:], offs3)
-        nc.sync.dma_start(out=cos_tab[1][:], in_=cos_rows[1, 0])
-        nc.sync.dma_start(out=sin_tab[1][:], in_=sin_rows[1, 0])
         for h in range(HALVES):
-            for j in range(2):
-                nc.sync.dma_start(out=old_sb[h][j][:], in_=old_rows[h, j])
+            nc.sync.dma_start(out=g_raw[h][:], in_=g_rows[:, :, h * EH:(h + 1) * EH])
+        for b in range(2):
+            nc.sync.dma_start(out=old_half[0][b][:], in_=old_rows[0, 0][:, 512 * b:512 * b + 512])
+        nc.sync.dma_start(out=cos_tab[1][:], in_=cos_rows[1, 0])
+        nc.sync.dma_start(out=old_half[1][0][:], in_=old_rows[0, 1][:, 0:512])
+        nc.sync.dma_start(out=sin_tab[1][:], in_=sin_rows[1, 0])
+        nc.sync.dma_start(out=old_half[1][1][:], in_=old_rows[0, 1][:, 512:1024])
+        for j in range(2):
+            nc.sync.dma_start(out=old_sb[j][:], in_=old_rows[1, j])
 
         ident = sb.tile([P, P], F32, name="ident", align_bytes=64)
         make_identity(nc, ident[:])
@@ -96,7 +101,14 @@ def tile_attend_gturnedvalues_kernel(tc, query, keys_words, keys_scales, qs, gro
         key_words = sb.tile([P, I], U32, name="key_words", align_bytes=64)
         nc.vector.tensor_copy(key_words[:], pool_words[:].indirect(key_list[:]))
 
-        neg_max = sb.tile([P, PACK], F32, name="neg_max")
+        cos_g = [sb.tile([P, I], F32, name="cos_g%d" % h, align_bytes=64) for h in range(HALVES)]
+        sin_g = [sb.tile([P, I], F32, name="sin_g%d" % h, align_bytes=64) for h in range(HALVES)]
+
+        def gather_by_distance(picked, table, lo=0, hi=I):
+            nc.vector.tensor_copy(picked[:, lo:hi], table[:].indirect(dist_list[:, lo // 16:hi // 16]))
+
+        gather_by_distance(cos_g[0], cos_tab[0])
+        neg_max = sb.tile([P, PACK], F32, name="neg_max", tag="cos0_then_max", align_bytes=64)
         row_sum = sb.tile([P, PACK], F32, name="row_sum")
         probs = sb.tile([P, PACK, I], F32, name="probs", align_bytes=64)
         for r in range(PACK):
@@ -111,42 +123,50 @@ def tile_attend_gturnedvalues_kernel(tc, query, keys_words, keys_scales, qs, gro
 
         g_bf, g_codes, g_scales = [], [], []
         for h in range(HALVES):
-            g_bf.append(sb.tile([P, 2, P, PACK], BF16, name="g_bf%d" % h, align_bytes=64))
+            g_bf.append(sb.tile([P, 2, P, PACK], BF16, name="g_bf%d" % h, tag="g_bf%d" % h, align_bytes=64))
             g_codes.append(sb.tile([P, EH], U32, name="g_codes%d" % h, align_bytes=64))
             g_scales.append(sb.tile([P, EH], U8, name="g_scales%d" % h, align_bytes=64))
             nc.scalar.copy(out=g_bf[h][:].rearrange("p j (c m) r -> p c r m j", m=2),
                            in_=g_raw[h][:].rearrange("p r (c m j) -> p c r m j", m=2, j=2))
 
-        cos_g, sin_g = [], []
-
-        def gather_angles(h):
-            cos_g.append(sb.tile([P, I], F32, name="cos_g%d" % h, align_bytes=64))
-            sin_g.append(sb.tile([P, I], F32, name="sin_g%d" % h, align_bytes=64))
-            nc.vector.tensor_copy(cos_g[h][:], cos_tab[h][:].indirect(dist_list[:]))
-            nc.vector.tensor_copy(sin_g[h][:], sin_tab[h][:].indirect(dist_list[:]))
-
-        gather_angles(0)
-        inv_sum = sb.tile([P, PACK], F32, name="inv_sum")
-        factor = sb.tile([P, PACK], F32, name="factor")
-        nc.vector.reciprocal(out=inv_sum[:], in_=row_sum[:])
-        nc.vector.tensor_tensor(out=factor[:], in0=inv_sum[:], in1=row_scale[:], op=ALU.mult)
-        w_bf = sb.tile([P, I, PACK], BF16, name="w_bf", align_bytes=64)
-        nc.vector.tensor_tensor(out=w_bf[:].rearrange("p (c m) r -> p c r m", m=4),
-                                in0=probs[:].rearrange("p r (c m) -> p c r m", m=4),
-                                in1=factor[:].unsqueeze(1).unsqueeze(3).to_broadcast([P, I // 4, PACK, 4]),
-                                op=ALU.mult)
-        w_codes = sb.tile([P, I], U32, name="w_codes", align_bytes=64)
-        w_scales = sb.tile([P, I], U8, name="w_scales", align_bytes=64)
-
         def quantise_grows(h):
             nc.vector.quantize_mx(out=g_codes[h][:].bitcast(FP8X4), scales=g_scales[h][:],
                                   in_=g_bf[h][:].rearrange("p j s r -> p (j s r)"))
 
+        turned_ps = {}
+
+        def turn_blocks(h, j, b, source, opens):
+            for k in range(4):
+                nc.tensor.matmul(turned_ps[h, j, b][:, k, :], lhsT=source[:, k * P:(k + 1) * P], rhs=ident[:], is_transpose=True,
+                                 start=(opens and k == 0), stop=(not opens and k == 3))
+
+        def turn_old(h, j, b):
+            turned_ps[h, j, b] = ps.tile([P, 4, P], F32, name="turned_ps", tag="bank%d" % (2 * j + b))
+            turn_blocks(h, j, b, old_half[j][b], True)
+
+        for b in range(2):
+            turn_old(0, 0, b)
+
+        inv_sum = sb.tile([P, PACK], F32, name="inv_sum")
+        factor = sb.tile([P, PACK], F32, name="factor")
+        w_bf = sb.tile([P, I, PACK], BF16, name="w_bf", align_bytes=64)
+        w_codes = sb.tile([P, I], U32, name="w_codes", tag="old000", align_bytes=64)
+        w_scales = sb.tile([P, I], U8, name="w_scales", align_bytes=64)
+        nc.vector.reciprocal(out=inv_sum[:], in_=row_sum[:])
+        gather_by_distance(sin_g[0], sin_tab[0], 0, I // 2)
+        nc.vector.tensor_tensor(out=factor[:], in0=inv_sum[:], in1=row_scale[:], op=ALU.mult)
+        gather_by_distance(sin_g[0], sin_tab[0], I // 2, I)
+        nc.vector.tensor_tensor(out=w_bf[:].rearrange("p (c m) r -> p c r m", m=4),
+                                in0=probs[:].rearrange("p r (c m) -> p c r m", m=4),
+                                in1=factor[:].unsqueeze(1).unsqueeze(3).to_broadcast([P, I // 4, PACK, 4]),
+                                op=ALU.mult)
         quantise_grows(0)
         nc.vector.quantize_mx(out=w_codes[:].bitcast(FP8X4), scales=w_scales[:],
                               in_=w_bf[:].rearrange("p i r -> p (i r)"))
+        gather_by_distance(cos_g[1], cos_tab[1])
+        quantise_grows(1)
 
-        dv = []
+        dv, by_cos, by_sin = [], {}, {}
 
         def second_product(h):
             dv.append(ps.tile([P, 2, I], F32, name="dv%d" % h))
@@ -156,34 +176,23 @@ def tile_attend_gturnedvalues_kernel(tc, query, keys_words, keys_scales, qs, gro
                                     lhsT_scale=g_scales[h][:, cols], rhs=w_codes[:].bitcast(FP8X4),
                                     rhs_scale=w_scales[:], start=True, stop=True)
 
-        def turn_and_place(h):
-            by_cos = sb.tile([P, 2, I], F32, name="by_cos%d" % h, align_bytes=64)
-            by_sin = sb.tile([P, 2, I], F32, name="by_sin%d" % h, align_bytes=64)
-            nc.vector.tensor_tensor(out=by_cos[:], in0=dv[h][:],
-                                    in1=cos_g[h][:].unsqueeze(1).to_broadcast([P, 2, I]), op=ALU.mult)
-            nc.vector.tensor_tensor(out=by_sin[:, 0, :], in0=dv[h][:, 1, :], in1=sin_g[h][:], op=ALU.mult)
-            nc.vector.scalar_tensor_tensor(out=by_sin[:, 1, :], in0=dv[h][:, 0, :], scalar=-1.0, in1=sin_g[h][:],
-                                           op0=ALU.mult, op1=ALU.mult)
-            for j in range(2):
-                nc.vector.tensor_tensor(placed[h][j][:].indirect(place_list[:]), by_cos[:, j, :], by_sin[:, j, :],
-                                        ALU.add)
+        def cos_term(h, j):
+            by_cos[h, j] = sb.tile([P, I], F32, name="by_cos%d%d" % (h, j), tag="by_cos%d" % j, align_bytes=64)
+            nc.vector.tensor_tensor(out=by_cos[h, j][:], in0=dv[h][:, j, :], in1=cos_g[h][:], op=ALU.mult)
 
-        turned_ps = {}
+        def sin_term(h, j):
+            tag = ("g_bf1", "by_sin1")[j]
+            by_sin[h, j] = sb.tile([P, I], F32, name="by_sin%d%d" % (h, j), tag=tag, align_bytes=64)
+            nc.vector.scalar_tensor_tensor(out=by_sin[h, j][:], in0=dv[h][:, 1 - j, :], scalar=(1.0, -1.0)[j],
+                                           in1=sin_g[h][:], op0=ALU.mult, op1=ALU.mult)
 
-        def turn_blocks(h, j, b, source, opens):
-            for k in range(4):
-                c0 = (4 * b + k) * P
-                nc.tensor.matmul(turned_ps[h, j, b][:, k, :], lhsT=source[:, c0:c0 + P], rhs=ident[:], is_transpose=True,
-                                 start=(opens and k == 0), stop=(not opens and k == 3))
-
-        def turn_old(h, j, b):
-            turned_ps[h, j, b] = ps.tile([P, 4, P], F32, name="turned_ps", tag="bank%d" % (2 * j + b))
-            turn_blocks(h, j, b, old_sb[h][j], True)
+        def place(h, j):
+            nc.vector.tensor_tensor(placed[h][j][:].indirect(place_list[:]), by_cos[h, j][:], by_sin[h, j][:], ALU.add)
 
         def add_on_tensor(h, j, halves):
             turned = {}
             for b in halves:
-                turn_blocks(h, j, b, placed[h][j], False)
+                turn_blocks(h, j, b, placed[h][j][:, b * 512:(b + 1) * 512], False)
                 turned[b] = sb.tile([P, 4, P], F32, name="turned", tag="turned", bufs=2, align_bytes=64)
                 nc.scalar.copy(out=turned[b][:], in_=turned_ps[h, j, b][:])
             for b in halves:
@@ -197,21 +206,27 @@ def tile_attend_gturnedvalues_kernel(tc, query, keys_words, keys_scales, qs, gro
         def add_on_vector(h, j, bounds):
             for lo, hi in zip(bounds, bounds[1:]):
                 total = sb.tile([P, hi - lo], F32, name="total_v%d%d_%d" % (h, j, lo), align_bytes=64)
-                nc.vector.tensor_tensor(out=total[:], in0=placed[h][j][:, lo:hi], in1=old_sb[h][j][:, lo:hi], op=ALU.add)
+                nc.vector.tensor_tensor(out=total[:], in0=placed[h][j][:, lo:hi], in1=old_sb[j][:, lo:hi], op=ALU.add)
                 nc.sync.dma_start(out=out_rows[h, j][:, lo:hi], in_=total[:])
 
         second_product(0)
-        gather_angles(1)
-        quantise_grows(1)
         second_product(1)
-        turn_and_place(0)
-        for j in range(2):
-            for b in range(2):
-                turn_old(0, j, b)
+        for b in range(2):
+            turn_old(0, 1, b)
+        sin_term(0, 0)
+        cos_term(0, 0)
+        cos_term(0, 1)
+        place(0, 0)
         add_on_tensor(0, 0, (0, 1))
-        turn_old(1, 0, 0)
+        sin_term(0, 1)
+        gather_by_distance(sin_g[1], sin_tab[1])
+        place(0, 1)
         add_on_tensor(0, 1, (0, 1))
-        turn_and_place(1)
-        add_on_tensor(1, 0, (0,))
-        add_on_vector(1, 0, (512, 1024))
+        sin_term(1, 0)
+        cos_term(1, 0)
+        cos_term(1, 1)
+        place(1, 0)
+        sin_term(1, 1)
+        add_on_vector(1, 0, (0, 1024))
+        place(1, 1)
         add_on_vector(1, 1, (0, 512, 768, 1024))

@@ -5,6 +5,7 @@ from concourse.masks import make_identity
 
 D, E, T, I, U, V, Q = 512, 512, 2048, 256, 1024, 512, 512
 FLOPS = 2 * D * Q * I + 2 * Q * E * I
+BYTES = 4 * D * Q + D * T + D // 32 * T + 4 * Q + 4 * Q * E + 4 * E * V + 8 * E * U + 3 * 128 * (I // 16) * 2
 
 F32 = mybir.dt.float32
 BF16 = mybir.dt.bfloat16
@@ -19,8 +20,14 @@ AX = mybir.AxisListType
 
 P = 128
 PACK = 4
+GROUP = 16
 HALVES = 2
+PAIR = 2
 EH = E // HALVES
+BANK = 512
+BANKS = U // BANK
+BLOCKS = BANK // P
+PIECES = ((0, 512, 1024), (0, 512, 768, 1024))
 
 
 def tile_attend_gturnedvalues_kernel(tc, query, keys_words, keys_scales, qs, grows, cosn, sinn, old,
@@ -30,73 +37,74 @@ def tile_attend_gturnedvalues_kernel(tc, query, keys_words, keys_scales, qs, gro
         sb = ctx.enter_context(tc.tile_pool(name="sb", bufs=1))
         ps = ctx.enter_context(tc.psum_pool(name="ps", bufs=1))
 
-        key_list = sb.tile([P, I // 16], U16, name="key_list")
-        dist_list = sb.tile([P, I // 16], U16, name="dist_list")
-        place_list = sb.tile([P, I // 16], U16, name="place_list")
+        key_list = sb.tile([P, I // GROUP], U16, name="key_list")
+        dist_list = sb.tile([P, I // GROUP], U16, name="dist_list")
+        place_list = sb.tile([P, I // GROUP], U16, name="place_list")
         pool_scales = sb.tile([P, T], U8, name="pool_scales", align_bytes=64)
         pool_words = sb.tile([P, T], U32, name="pool_words", align_bytes=64)
         q_raw = sb.tile([P, PACK, Q], F32, name="q_raw", align_bytes=64)
         row_scale = sb.tile([P, PACK], F32, name="row_scale")
         g_raw = [sb.tile([P, PACK, EH], F32, name="g_raw%d" % h, align_bytes=64) for h in range(HALVES)]
-        cos_tab = [sb.tile([P, V], F32, name="cos_tab%d" % h, tag=("cos0_then_max", "cos1")[h], align_bytes=64)
+        cos_tab = [sb.tile([P, V], F32, name="cos_tab%d" % h, tag="cos_tab%d" % h, align_bytes=64)
                    for h in range(HALVES)]
         sin_tab = [sb.tile([P, V], F32, name="sin_tab%d" % h, align_bytes=64) for h in range(HALVES)]
-        old_half = [[sb.tile([P, U // 2], F32, name="old0%d%d" % (j, b), tag="old0%d%d" % (j, b), align_bytes=64) for b in range(2)] for j in range(2)]
-        old_sb = [sb.tile([P, U], F32, name="old1%d" % j, align_bytes=64) for j in range(2)]
-        placed = [[sb.tile([P, U], F32, name="placed%d%d" % (h, j), align_bytes=64) for j in range(2)] for h in range(HALVES)]
-
-        warm_in = sb.tile([P, 1], F32, name="warm_in")
-        warm_out = sb.tile([P, 1], F32, name="warm_out")
+        old_first = [[sb.tile([P, BANK], F32, name="old0%d%d" % (j, b), tag="old0%d%d" % (j, b), align_bytes=64)
+                      for b in range(BANKS)] for j in range(PAIR)]
+        old_second = [sb.tile([P, U], F32, name="old1%d" % j, align_bytes=64) for j in range(PAIR)]
+        placed = [[sb.tile([P, U], F32, name="placed%d%d" % (h, j), align_bytes=64) for j in range(PAIR)]
+                  for h in range(HALVES)]
 
         nc.gpsimd.memset(pool_scales[:].bitcast(I32), 0)
-        nc.gpsimd.memset(warm_in[:], 0.0)
-        nc.scalar.activation(out=warm_out[:], in_=warm_in[:], func=ACT.Exp)
 
-        nc.sync.dma_start(out=q_raw[:], in_=query.rearrange("(p j) q -> p j q", j=PACK))
-        for r in range(4):
-            nc.sync.dma_start(out=pool_scales[r:P:32, :].bitcast(I32), in_=keys_scales[0, r:16:4, :].bitcast(I32))
+        g_rows = grows.rearrange("(p r) e -> p r e", r=PACK)
+        cos_rows = cosn.rearrange("(h p j) v -> h j p v", h=HALVES, j=PAIR)
+        sin_rows = sinn.rearrange("(h p j) v -> h j p v", h=HALVES, j=PAIR)
+        old_rows = old.rearrange("(h p j) u -> h j p u", h=HALVES, j=PAIR)
+        out_rows = out.rearrange("(h p j) u -> h j p u", h=HALVES, j=PAIR)
+
+        def bank_cols(b):
+            return slice(b * BANK, (b + 1) * BANK)
+
+        nc.sync.dma_start(out=q_raw[:], in_=query.rearrange("(p t) q -> p t q", t=PACK))
+        for row in range(4):
+            nc.sync.dma_start(out=pool_scales[row:P:32, :].bitcast(I32),
+                              in_=keys_scales[0, row:16:4, :].bitcast(I32))
         nc.sync.dma_start(key_list[:], offs)
         nc.sync.dma_start(dist_list[:], offs2)
         nc.sync.dma_start(out=pool_words[:].bitcast(I32),
-                          in_=keys_words[0].rearrange("p t r -> p (t r)").bitcast(I32))
-        g_rows = grows.rearrange("(p r) e -> p r e", r=PACK)
-        cos_rows = cosn.rearrange("(h p j) v -> h j p v", h=HALVES, j=2)
-        sin_rows = sinn.rearrange("(h p j) v -> h j p v", h=HALVES, j=2)
-        old_rows = old.rearrange("(h p j) u -> h j p u", h=HALVES, j=2)
-        out_rows = out.rearrange("(h p j) u -> h j p u", h=HALVES, j=2)
+                          in_=keys_words[0].rearrange("p token t -> p (token t)").bitcast(I32))
         nc.sync.dma_start(out=cos_tab[0][:], in_=cos_rows[0, 0])
         nc.sync.dma_start(out=sin_tab[0][:], in_=sin_rows[0, 0])
         nc.sync.dma_start(out=row_scale[:], in_=qs.rearrange("(p r) o -> p (r o)", r=PACK))
         nc.sync.dma_start(place_list[:], offs3)
         for h in range(HALVES):
             nc.sync.dma_start(out=g_raw[h][:], in_=g_rows[:, :, h * EH:(h + 1) * EH])
-        for b in range(2):
-            nc.sync.dma_start(out=old_half[0][b][:], in_=old_rows[0, 0][:, 512 * b:512 * b + 512])
-        nc.sync.dma_start(out=cos_tab[1][:], in_=cos_rows[1, 0])
-        nc.sync.dma_start(out=old_half[1][0][:], in_=old_rows[0, 1][:, 0:512])
-        nc.sync.dma_start(out=sin_tab[1][:], in_=sin_rows[1, 0])
-        nc.sync.dma_start(out=old_half[1][1][:], in_=old_rows[0, 1][:, 512:1024])
-        for j in range(2):
-            nc.sync.dma_start(out=old_sb[j][:], in_=old_rows[1, j])
+        for b in range(BANKS):
+            nc.sync.dma_start(out=old_first[0][b][:], in_=old_rows[0, 0][:, bank_cols(b)])
+        for b, (table, rows) in enumerate(((cos_tab, cos_rows), (sin_tab, sin_rows))):
+            nc.sync.dma_start(out=table[1][:], in_=rows[1, 0])
+            nc.sync.dma_start(out=old_first[1][b][:], in_=old_rows[0, 1][:, bank_cols(b)])
+        for j in range(PAIR):
+            nc.sync.dma_start(out=old_second[j][:], in_=old_rows[1, j])
 
         ident = sb.tile([P, P], F32, name="ident", align_bytes=64)
         make_identity(nc, ident[:])
         for h in range(HALVES):
-            for j in range(2):
+            for j in range(PAIR):
                 nc.vector.memset(placed[h][j][:], 0.0)
 
-        q_cols = q_raw[:].rearrange("p j (s r) -> p s j r", r=PACK)
+        q_cols = q_raw[:].rearrange("p t (s r) -> p s t r", r=PACK)
         q_codes, q_scales, q_bf = [], [], []
         for a, copy in enumerate((nc.vector.tensor_copy, nc.scalar.copy)):
             q_bf.append(sb.tile([P, 2, P, PACK], BF16, name="q_bf%d" % a, align_bytes=64))
-            copy(out=q_bf[a][:].rearrange("p r s j -> p s j r"), in_=q_cols[:, :, :, 2 * a:2 * a + 2])
+            copy(out=q_bf[a][:].rearrange("p r s t -> p s t r"), in_=q_cols[:, :, :, 2 * a:2 * a + 2])
         key_scales = sb.tile([P, I], U8, name="key_scales", align_bytes=64)
         nc.vector.tensor_copy(key_scales[:], pool_scales[:].indirect(key_list[:]))
-        for a in range(2):
+        for a in range(len(q_bf)):
             q_codes.append(sb.tile([P, 2 * P], U32, name="q_codes%d" % a, align_bytes=64))
             q_scales.append(sb.tile([P, 2 * P], U8, name="q_scales%d" % a, align_bytes=64))
             nc.vector.quantize_mx(out=q_codes[a][:].bitcast(FP8X4), scales=q_scales[a][:],
-                                  in_=q_bf[a][:].rearrange("p r s j -> p (r s j)"))
+                                  in_=q_bf[a][:].rearrange("p r s t -> p (r s t)"))
 
         key_words = sb.tile([P, I], U32, name="key_words", align_bytes=64)
         nc.vector.tensor_copy(key_words[:], pool_words[:].indirect(key_list[:]))
@@ -105,10 +113,10 @@ def tile_attend_gturnedvalues_kernel(tc, query, keys_words, keys_scales, qs, gro
         sin_g = [sb.tile([P, I], F32, name="sin_g%d" % h, align_bytes=64) for h in range(HALVES)]
 
         def gather_by_distance(picked, table, lo=0, hi=I):
-            nc.vector.tensor_copy(picked[:, lo:hi], table[:].indirect(dist_list[:, lo // 16:hi // 16]))
+            nc.vector.tensor_copy(picked[:, lo:hi], table[:].indirect(dist_list[:, lo // GROUP:hi // GROUP]))
 
         gather_by_distance(cos_g[0], cos_tab[0])
-        neg_max = sb.tile([P, PACK], F32, name="neg_max", tag="cos0_then_max", align_bytes=64)
+        neg_max = sb.tile([P, PACK], F32, name="neg_max", tag="cos_tab0", align_bytes=64)
         row_sum = sb.tile([P, PACK], F32, name="row_sum")
         probs = sb.tile([P, PACK, I], F32, name="probs", align_bytes=64)
         for r in range(PACK):
@@ -123,29 +131,29 @@ def tile_attend_gturnedvalues_kernel(tc, query, keys_words, keys_scales, qs, gro
 
         g_bf, g_codes, g_scales = [], [], []
         for h in range(HALVES):
-            g_bf.append(sb.tile([P, 2, P, PACK], BF16, name="g_bf%d" % h, tag="g_bf%d" % h, align_bytes=64))
+            g_bf.append(sb.tile([P, PAIR, P, PACK], BF16, name="g_bf%d" % h, tag="g_bf%d" % h, align_bytes=64))
             g_codes.append(sb.tile([P, EH], U32, name="g_codes%d" % h, align_bytes=64))
             g_scales.append(sb.tile([P, EH], U8, name="g_scales%d" % h, align_bytes=64))
             nc.scalar.copy(out=g_bf[h][:].rearrange("p j (c m) r -> p c r m j", m=2),
-                           in_=g_raw[h][:].rearrange("p r (c m j) -> p c r m j", m=2, j=2))
+                           in_=g_raw[h][:].rearrange("p r (c m j) -> p c r m j", m=2, j=PAIR))
 
         def quantise_grows(h):
             nc.vector.quantize_mx(out=g_codes[h][:].bitcast(FP8X4), scales=g_scales[h][:],
                                   in_=g_bf[h][:].rearrange("p j s r -> p (j s r)"))
 
-        turned_ps = {}
+        sum_ps = {}
 
-        def turn_blocks(h, j, b, source, opens):
-            for k in range(4):
-                nc.tensor.matmul(turned_ps[h, j, b][:, k, :], lhsT=source[:, k * P:(k + 1) * P], rhs=ident[:], is_transpose=True,
-                                 start=(opens and k == 0), stop=(not opens and k == 3))
+        def transpose_blocks(j, b, source, opens):
+            for k in range(BLOCKS):
+                nc.tensor.matmul(sum_ps[j, b][:, k, :], lhsT=source[:, k * P:(k + 1) * P], rhs=ident[:],
+                                 is_transpose=True, start=(opens and k == 0), stop=(not opens and k == BLOCKS - 1))
 
-        def turn_old(h, j, b):
-            turned_ps[h, j, b] = ps.tile([P, 4, P], F32, name="turned_ps", tag="bank%d" % (2 * j + b))
-            turn_blocks(h, j, b, old_half[j][b], True)
+        def open_sum_with_old(j):
+            for b in range(BANKS):
+                sum_ps[j, b] = ps.tile([P, BLOCKS, P], F32, name="sum_ps", tag="bank%d" % (BANKS * j + b))
+                transpose_blocks(j, b, old_first[j][b], True)
 
-        for b in range(2):
-            turn_old(0, 0, b)
+        open_sum_with_old(0)
 
         inv_sum = sb.tile([P, PACK], F32, name="inv_sum")
         factor = sb.tile([P, PACK], F32, name="factor")
@@ -156,8 +164,8 @@ def tile_attend_gturnedvalues_kernel(tc, query, keys_words, keys_scales, qs, gro
         gather_by_distance(sin_g[0], sin_tab[0], 0, I // 2)
         nc.vector.tensor_tensor(out=factor[:], in0=inv_sum[:], in1=row_scale[:], op=ALU.mult)
         gather_by_distance(sin_g[0], sin_tab[0], I // 2, I)
-        nc.vector.tensor_tensor(out=w_bf[:].rearrange("p (c m) r -> p c r m", m=4),
-                                in0=probs[:].rearrange("p r (c m) -> p c r m", m=4),
+        nc.vector.tensor_tensor(out=w_bf[:].rearrange("p (c n) r -> p c r n", n=4),
+                                in0=probs[:].rearrange("p r (c n) -> p c r n", n=4),
                                 in1=factor[:].unsqueeze(1).unsqueeze(3).to_broadcast([P, I // 4, PACK, 4]),
                                 op=ALU.mult)
         quantise_grows(0)
@@ -166,67 +174,66 @@ def tile_attend_gturnedvalues_kernel(tc, query, keys_words, keys_scales, qs, gro
         gather_by_distance(cos_g[1], cos_tab[1])
         quantise_grows(1)
 
-        dv, by_cos, by_sin = [], {}, {}
-
-        def second_product(h):
-            dv.append(ps.tile([P, 2, I], F32, name="dv%d" % h))
-            for j in range(2):
+        dv = []
+        for h in range(HALVES):
+            dv.append(ps.tile([P, PAIR, I], F32, name="dv%d" % h))
+            for j in range(PAIR):
                 cols = slice(j * P, (j + 1) * P)
                 nc.tensor.matmul_mx(out=dv[h][:, j, :], lhsT=g_codes[h][:, cols].bitcast(FP8X4),
                                     lhsT_scale=g_scales[h][:, cols], rhs=w_codes[:].bitcast(FP8X4),
                                     rhs_scale=w_scales[:], start=True, stop=True)
+        open_sum_with_old(1)
+
+        by_cos, by_sin = {}, {}
 
         def cos_term(h, j):
             by_cos[h, j] = sb.tile([P, I], F32, name="by_cos%d%d" % (h, j), tag="by_cos%d" % j, align_bytes=64)
             nc.vector.tensor_tensor(out=by_cos[h, j][:], in0=dv[h][:, j, :], in1=cos_g[h][:], op=ALU.mult)
 
         def sin_term(h, j):
-            tag = ("g_bf1", "by_sin1")[j]
-            by_sin[h, j] = sb.tile([P, I], F32, name="by_sin%d%d" % (h, j), tag=tag, align_bytes=64)
+            by_sin[h, j] = sb.tile([P, I], F32, name="by_sin%d%d" % (h, j), tag=("g_bf1", "by_sin1")[j],
+                                   align_bytes=64)
             nc.vector.scalar_tensor_tensor(out=by_sin[h, j][:], in0=dv[h][:, 1 - j, :], scalar=(1.0, -1.0)[j],
                                            in1=sin_g[h][:], op0=ALU.mult, op1=ALU.mult)
 
         def place(h, j):
             nc.vector.tensor_tensor(placed[h][j][:].indirect(place_list[:]), by_cos[h, j][:], by_sin[h, j][:], ALU.add)
 
-        def add_on_tensor(h, j, halves):
-            turned = {}
-            for b in halves:
-                turn_blocks(h, j, b, placed[h][j][:, b * 512:(b + 1) * 512], False)
-                turned[b] = sb.tile([P, 4, P], F32, name="turned", tag="turned", bufs=2, align_bytes=64)
-                nc.scalar.copy(out=turned[b][:], in_=turned_ps[h, j, b][:])
-            for b in halves:
-                back_ps = ps.tile([P, 4, P], F32, name="back_ps", tag="back", bufs=2)
-                for k in range(4):
-                    nc.tensor.transpose(back_ps[:, k, :], turned[b][:, k, :], ident[:])
-                total = sb.tile([P, 4 * P], F32, name="total_t%d%d%d" % (h, j, b), align_bytes=64)
-                nc.scalar.copy(out=total[:], in_=back_ps[:].rearrange("p k c -> p (k c)"))
-                nc.scalar.dma_start(out=out_rows[h, j][:, b * 512:(b + 1) * 512], in_=total[:])
+        def add_old_on_tensor(j):
+            sum_sb = []
+            for b in range(BANKS):
+                transpose_blocks(j, b, placed[0][j][:, bank_cols(b)], False)
+                sum_sb.append(sb.tile([P, BLOCKS, P], F32, name="sum_sb", tag="sum_sb", bufs=BANKS, align_bytes=64))
+                nc.scalar.copy(out=sum_sb[b][:], in_=sum_ps[j, b][:])
+            for b in range(BANKS):
+                back_ps = ps.tile([P, BLOCKS, P], F32, name="back_ps", tag="back_ps", bufs=BANKS)
+                for k in range(BLOCKS):
+                    nc.tensor.transpose(back_ps[:, k, :], sum_sb[b][:, k, :], ident[:])
+                total = sb.tile([P, BANK], F32, name="total0%d%d" % (j, b), align_bytes=64)
+                nc.scalar.copy(out=total[:], in_=back_ps[:].rearrange("p k u -> p (k u)"))
+                nc.scalar.dma_start(out=out_rows[0, j][:, bank_cols(b)], in_=total[:])
 
-        def add_on_vector(h, j, bounds):
-            for lo, hi in zip(bounds, bounds[1:]):
-                total = sb.tile([P, hi - lo], F32, name="total_v%d%d_%d" % (h, j, lo), align_bytes=64)
-                nc.vector.tensor_tensor(out=total[:], in0=placed[h][j][:, lo:hi], in1=old_sb[j][:, lo:hi], op=ALU.add)
-                nc.sync.dma_start(out=out_rows[h, j][:, lo:hi], in_=total[:])
+        def add_old_on_vector(j):
+            for lo, hi in zip(PIECES[j], PIECES[j][1:]):
+                total = sb.tile([P, hi - lo], F32, name="total1%d_%d" % (j, lo), align_bytes=64)
+                nc.vector.tensor_tensor(out=total[:], in0=placed[1][j][:, lo:hi], in1=old_second[j][:, lo:hi],
+                                        op=ALU.add)
+                nc.sync.dma_start(out=out_rows[1, j][:, lo:hi], in_=total[:])
 
-        second_product(0)
-        second_product(1)
-        for b in range(2):
-            turn_old(0, 1, b)
         sin_term(0, 0)
         cos_term(0, 0)
         cos_term(0, 1)
         place(0, 0)
-        add_on_tensor(0, 0, (0, 1))
+        add_old_on_tensor(0)
         sin_term(0, 1)
         gather_by_distance(sin_g[1], sin_tab[1])
         place(0, 1)
-        add_on_tensor(0, 1, (0, 1))
+        add_old_on_tensor(1)
         sin_term(1, 0)
         cos_term(1, 0)
         cos_term(1, 1)
         place(1, 0)
         sin_term(1, 1)
-        add_on_vector(1, 0, (0, 1024))
+        add_old_on_vector(0)
         place(1, 1)
-        add_on_vector(1, 1, (0, 512, 768, 1024))
+        add_old_on_vector(1)

from contextlib import ExitStack

import concourse.mybir as mybir
from concourse.masks import make_identity

D, E, T, I, U, V, Q = 512, 512, 2048, 256, 1024, 512, 512
FLOPS = 2 * D * Q * I + 2 * Q * E * I
BYTES = 4 * D * Q + D * T + D // 32 * T + 4 * Q + 4 * Q * E + 4 * E * V + 8 * E * U + 3 * 128 * (I // 16) * 2

F32 = mybir.dt.float32
BF16 = mybir.dt.bfloat16
I32 = mybir.dt.int32
U32 = mybir.dt.uint32
U16 = mybir.dt.uint16
U8 = mybir.dt.uint8
FP8X4 = mybir.dt.float8_e4m3fn_x4
ALU = mybir.AluOpType
ACT = mybir.ActivationFunctionType
AX = mybir.AxisListType

P = 128
PACK = 4
GROUP = 16
HALVES = 2
PAIR = 2
EH = E // HALVES
BANK = 512
BANKS = U // BANK
BLOCKS = BANK // P
PIECES = ((0, 512, 1024), (0, 512, 768, 1024))


def tile_attend_gturnedvalues_kernel(tc, query, keys_words, keys_scales, qs, grows, cosn, sinn, old,
                                      offs, offs2, offs3, out):
    nc = tc.nc
    with ExitStack() as ctx:
        sb = ctx.enter_context(tc.tile_pool(name="sb", bufs=1))
        ps = ctx.enter_context(tc.psum_pool(name="ps", bufs=1))

        key_list = sb.tile([P, I // GROUP], U16, name="key_list")
        dist_list = sb.tile([P, I // GROUP], U16, name="dist_list")
        place_list = sb.tile([P, I // GROUP], U16, name="place_list")
        pool_scales = sb.tile([P, T], U8, name="pool_scales", align_bytes=64)
        pool_words = sb.tile([P, T], U32, name="pool_words", align_bytes=64)
        q_raw = sb.tile([P, PACK, Q], F32, name="q_raw", align_bytes=64)
        row_scale = sb.tile([P, PACK], F32, name="row_scale")
        g_raw = [sb.tile([P, PACK, EH], F32, name="g_raw%d" % h, align_bytes=64) for h in range(HALVES)]
        cos_tab = [sb.tile([P, V], F32, name="cos_tab%d" % h, tag="cos_tab%d" % h, align_bytes=64)
                   for h in range(HALVES)]
        sin_tab = [sb.tile([P, V], F32, name="sin_tab%d" % h, align_bytes=64) for h in range(HALVES)]
        old_first = [[sb.tile([P, BANK], F32, name="old0%d%d" % (j, b), tag="old0%d%d" % (j, b), align_bytes=64)
                      for b in range(BANKS)] for j in range(PAIR)]
        old_second = [sb.tile([P, U], F32, name="old1%d" % j, align_bytes=64) for j in range(PAIR)]
        placed = [[sb.tile([P, U], F32, name="placed%d%d" % (h, j), align_bytes=64) for j in range(PAIR)]
                  for h in range(HALVES)]

        nc.gpsimd.memset(pool_scales[:].bitcast(I32), 0)

        g_rows = grows.rearrange("(p r) e -> p r e", r=PACK)
        cos_rows = cosn.rearrange("(h p j) v -> h j p v", h=HALVES, j=PAIR)
        sin_rows = sinn.rearrange("(h p j) v -> h j p v", h=HALVES, j=PAIR)
        old_rows = old.rearrange("(h p j) u -> h j p u", h=HALVES, j=PAIR)
        out_rows = out.rearrange("(h p j) u -> h j p u", h=HALVES, j=PAIR)

        def bank_cols(b):
            return slice(b * BANK, (b + 1) * BANK)

        nc.sync.dma_start(out=q_raw[:], in_=query.rearrange("(p t) q -> p t q", t=PACK))
        for row in range(4):
            nc.sync.dma_start(out=pool_scales[row:P:32, :].bitcast(I32),
                              in_=keys_scales[0, row:16:4, :].bitcast(I32))
        nc.sync.dma_start(key_list[:], offs)
        nc.sync.dma_start(dist_list[:], offs2)
        nc.sync.dma_start(out=pool_words[:].bitcast(I32),
                          in_=keys_words[0].rearrange("p token t -> p (token t)").bitcast(I32))
        nc.sync.dma_start(out=cos_tab[0][:], in_=cos_rows[0, 0])
        nc.sync.dma_start(out=sin_tab[0][:], in_=sin_rows[0, 0])
        nc.sync.dma_start(out=row_scale[:], in_=qs.rearrange("(p r) o -> p (r o)", r=PACK))
        nc.sync.dma_start(place_list[:], offs3)
        for h in range(HALVES):
            nc.sync.dma_start(out=g_raw[h][:], in_=g_rows[:, :, h * EH:(h + 1) * EH])
        for b in range(BANKS):
            nc.sync.dma_start(out=old_first[0][b][:], in_=old_rows[0, 0][:, bank_cols(b)])
        for b, (table, rows) in enumerate(((cos_tab, cos_rows), (sin_tab, sin_rows))):
            nc.sync.dma_start(out=table[1][:], in_=rows[1, 0])
            nc.sync.dma_start(out=old_first[1][b][:], in_=old_rows[0, 1][:, bank_cols(b)])
        for j in range(PAIR):
            nc.sync.dma_start(out=old_second[j][:], in_=old_rows[1, j])

        ident = sb.tile([P, P], F32, name="ident", align_bytes=64)
        make_identity(nc, ident[:])
        for h in range(HALVES):
            for j in range(PAIR):
                nc.vector.memset(placed[h][j][:], 0.0)

        q_cols = q_raw[:].rearrange("p t (s r) -> p s t r", r=PACK)
        q_codes, q_scales, q_bf = [], [], []
        for a, copy in enumerate((nc.vector.tensor_copy, nc.scalar.copy)):
            q_bf.append(sb.tile([P, 2, P, PACK], BF16, name="q_bf%d" % a, align_bytes=64))
            copy(out=q_bf[a][:].rearrange("p r s t -> p s t r"), in_=q_cols[:, :, :, 2 * a:2 * a + 2])
        key_scales = sb.tile([P, I], U8, name="key_scales", align_bytes=64)
        nc.vector.tensor_copy(key_scales[:], pool_scales[:].indirect(key_list[:]))
        for a in range(len(q_bf)):
            q_codes.append(sb.tile([P, 2 * P], U32, name="q_codes%d" % a, align_bytes=64))
            q_scales.append(sb.tile([P, 2 * P], U8, name="q_scales%d" % a, align_bytes=64))
            nc.vector.quantize_mx(out=q_codes[a][:].bitcast(FP8X4), scales=q_scales[a][:],
                                  in_=q_bf[a][:].rearrange("p r s t -> p (r s t)"))

        key_words = sb.tile([P, I], U32, name="key_words", align_bytes=64)
        nc.vector.tensor_copy(key_words[:], pool_words[:].indirect(key_list[:]))

        cos_g = [sb.tile([P, I], F32, name="cos_g%d" % h, align_bytes=64) for h in range(HALVES)]
        sin_g = [sb.tile([P, I], F32, name="sin_g%d" % h, align_bytes=64) for h in range(HALVES)]

        def gather_by_distance(picked, table, lo=0, hi=I):
            nc.vector.tensor_copy(picked[:, lo:hi], table[:].indirect(dist_list[:, lo // GROUP:hi // GROUP]))

        gather_by_distance(cos_g[0], cos_tab[0])
        neg_max = sb.tile([P, PACK], F32, name="neg_max", tag="cos_tab0", align_bytes=64)
        row_sum = sb.tile([P, PACK], F32, name="row_sum")
        probs = sb.tile([P, PACK, I], F32, name="probs", align_bytes=64)
        for r in range(PACK):
            cols = slice(r % 2 * P, (r % 2 + 1) * P)
            scores = ps.tile([P, I], F32, name="scores%d" % r, tag="bank%d" % r)
            nc.tensor.matmul_mx(out=scores[:], lhsT=q_codes[r // 2][:, cols].bitcast(FP8X4),
                                lhsT_scale=q_scales[r // 2][:, cols],
                                rhs=key_words[:].bitcast(FP8X4), rhs_scale=key_scales[:], start=True, stop=True)
            nc.vector.tensor_reduce(out=neg_max[:, r:r + 1], in_=scores[:], axis=AX.X, op=ALU.max, negate=True)
            nc.scalar.activation(out=probs[:, r, :], in_=scores[:], func=ACT.Exp, bias=neg_max[:, r:r + 1],
                                 accum_out=row_sum[:, r:r + 1])

        g_bf, g_codes, g_scales = [], [], []
        for h in range(HALVES):
            g_bf.append(sb.tile([P, PAIR, P, PACK], BF16, name="g_bf%d" % h, tag="g_bf%d" % h, align_bytes=64))
            g_codes.append(sb.tile([P, EH], U32, name="g_codes%d" % h, align_bytes=64))
            g_scales.append(sb.tile([P, EH], U8, name="g_scales%d" % h, align_bytes=64))
            nc.scalar.copy(out=g_bf[h][:].rearrange("p j (c m) r -> p c r m j", m=2),
                           in_=g_raw[h][:].rearrange("p r (c m j) -> p c r m j", m=2, j=PAIR))

        def quantise_grows(h):
            nc.vector.quantize_mx(out=g_codes[h][:].bitcast(FP8X4), scales=g_scales[h][:],
                                  in_=g_bf[h][:].rearrange("p j s r -> p (j s r)"))

        sum_ps = {}

        def transpose_blocks(j, b, source, opens):
            for k in range(BLOCKS):
                nc.tensor.matmul(sum_ps[j, b][:, k, :], lhsT=source[:, k * P:(k + 1) * P], rhs=ident[:],
                                 is_transpose=True, start=(opens and k == 0), stop=(not opens and k == BLOCKS - 1))

        def open_sum_with_old(j):
            for b in range(BANKS):
                sum_ps[j, b] = ps.tile([P, BLOCKS, P], F32, name="sum_ps", tag="bank%d" % (BANKS * j + b))
                transpose_blocks(j, b, old_first[j][b], True)

        open_sum_with_old(0)

        inv_sum = sb.tile([P, PACK], F32, name="inv_sum")
        factor = sb.tile([P, PACK], F32, name="factor")
        w_bf = sb.tile([P, I, PACK], BF16, name="w_bf", align_bytes=64)
        w_codes = sb.tile([P, I], U32, name="w_codes", tag="old000", align_bytes=64)
        w_scales = sb.tile([P, I], U8, name="w_scales", align_bytes=64)
        nc.vector.reciprocal(out=inv_sum[:], in_=row_sum[:])
        gather_by_distance(sin_g[0], sin_tab[0], 0, I // 2)
        nc.vector.tensor_tensor(out=factor[:], in0=inv_sum[:], in1=row_scale[:], op=ALU.mult)
        gather_by_distance(sin_g[0], sin_tab[0], I // 2, I)
        nc.vector.tensor_tensor(out=w_bf[:].rearrange("p (c n) r -> p c r n", n=4),
                                in0=probs[:].rearrange("p r (c n) -> p c r n", n=4),
                                in1=factor[:].unsqueeze(1).unsqueeze(3).to_broadcast([P, I // 4, PACK, 4]),
                                op=ALU.mult)
        quantise_grows(0)
        nc.vector.quantize_mx(out=w_codes[:].bitcast(FP8X4), scales=w_scales[:],
                              in_=w_bf[:].rearrange("p i r -> p (i r)"))
        gather_by_distance(cos_g[1], cos_tab[1])
        quantise_grows(1)

        dv = []
        for h in range(HALVES):
            dv.append(ps.tile([P, PAIR, I], F32, name="dv%d" % h))
            for j in range(PAIR):
                cols = slice(j * P, (j + 1) * P)
                nc.tensor.matmul_mx(out=dv[h][:, j, :], lhsT=g_codes[h][:, cols].bitcast(FP8X4),
                                    lhsT_scale=g_scales[h][:, cols], rhs=w_codes[:].bitcast(FP8X4),
                                    rhs_scale=w_scales[:], start=True, stop=True)
        open_sum_with_old(1)

        by_cos, by_sin = {}, {}

        def cos_term(h, j):
            by_cos[h, j] = sb.tile([P, I], F32, name="by_cos%d%d" % (h, j), tag="by_cos%d" % j, align_bytes=64)
            nc.vector.tensor_tensor(out=by_cos[h, j][:], in0=dv[h][:, j, :], in1=cos_g[h][:], op=ALU.mult)

        def sin_term(h, j):
            by_sin[h, j] = sb.tile([P, I], F32, name="by_sin%d%d" % (h, j), tag=("g_bf1", "by_sin1")[j],
                                   align_bytes=64)
            nc.vector.scalar_tensor_tensor(out=by_sin[h, j][:], in0=dv[h][:, 1 - j, :], scalar=(1.0, -1.0)[j],
                                           in1=sin_g[h][:], op0=ALU.mult, op1=ALU.mult)

        def place(h, j):
            nc.vector.tensor_tensor(placed[h][j][:].indirect(place_list[:]), by_cos[h, j][:], by_sin[h, j][:], ALU.add)

        def add_old_on_tensor(j):
            sum_sb = []
            for b in range(BANKS):
                transpose_blocks(j, b, placed[0][j][:, bank_cols(b)], False)
                sum_sb.append(sb.tile([P, BLOCKS, P], F32, name="sum_sb", tag="sum_sb", bufs=BANKS, align_bytes=64))
                nc.scalar.copy(out=sum_sb[b][:], in_=sum_ps[j, b][:])
            for b in range(BANKS):
                back_ps = ps.tile([P, BLOCKS, P], F32, name="back_ps", tag="back_ps", bufs=BANKS)
                for k in range(BLOCKS):
                    nc.tensor.transpose(back_ps[:, k, :], sum_sb[b][:, k, :], ident[:])
                total = sb.tile([P, BANK], F32, name="total0%d%d" % (j, b), align_bytes=64)
                nc.scalar.copy(out=total[:], in_=back_ps[:].rearrange("p k u -> p (k u)"))
                nc.scalar.dma_start(out=out_rows[0, j][:, bank_cols(b)], in_=total[:])

        def add_old_on_vector(j):
            for lo, hi in zip(PIECES[j], PIECES[j][1:]):
                total = sb.tile([P, hi - lo], F32, name="total1%d_%d" % (j, lo), align_bytes=64)
                nc.vector.tensor_tensor(out=total[:], in0=placed[1][j][:, lo:hi], in1=old_second[j][:, lo:hi],
                                        op=ALU.add)
                nc.sync.dma_start(out=out_rows[1, j][:, lo:hi], in_=total[:])

        sin_term(0, 0)
        cos_term(0, 0)
        cos_term(0, 1)
        place(0, 0)
        add_old_on_tensor(0)
        sin_term(0, 1)
        gather_by_distance(sin_g[1], sin_tab[1])
        place(0, 1)
        add_old_on_tensor(1)
        sin_term(1, 0)
        cos_term(1, 0)
        cos_term(1, 1)
        place(1, 0)
        sin_term(1, 1)
        add_old_on_vector(0)
        place(1, 1)
        add_old_on_vector(1)
